import numpy as np
import ml_dtypes


def mxq(x, axis, fmt="e4m3"):
    dtype, down = {"e4m3": (ml_dtypes.float8_e4m3fn, 7), "e5m2": (ml_dtypes.float8_e5m2, 14)}[fmt]
    v = np.moveaxis(np.asarray(x, np.float32).astype(ml_dtypes.bfloat16).astype(np.float64), axis, -1)
    blocks = v.reshape(v.shape[:-1] + (-1, 32))
    amax = np.abs(blocks).max(-1, keepdims=True)
    byte = np.maximum(np.where(amax > 0, np.frexp(amax)[1] - 1 + 127, 0) - down, 1)
    scale = np.exp2(byte - 127.0)
    codes = (blocks / scale).astype(np.float32).astype(dtype).astype(np.float64)
    return np.moveaxis((codes * scale).reshape(v.shape), -1, axis)


WIDE = False


def mx_kscale(k):
    if not WIDE:
        return np.ones(k)
    levels = np.array([10, -10, 5, -5, 0])
    if k % 512:
        return np.exp2(np.random.permutation(np.resize(levels, k // 32))).repeat(32)
    a = np.empty((k // 512, 16))
    for p in range(k // 512):
        a[p, :8] = np.random.permutation(np.resize(levels, 8))
        for g in range(8):
            far = levels[np.abs(levels - a[p, g]) >= 10]
            a[p, g + 8] = far[np.random.randint(len(far))]
    return np.exp2(a.ravel()).repeat(32)


def f64(x):
    return np.asarray(x).astype(np.float64)


def striped(idx):
    return np.tile(idx.reshape(-1, 16).T, (8, 1)).astype(np.uint16)


def unstriped(offs):
    return offs[:16].T.reshape(-1).astype(np.int64)


E2M1 = np.array([0.0, 0.5, 1.0, 1.5, 2.0, 3.0, 4.0, 6.0, -0.0, -0.5, -1.0, -1.5, -2.0, -3.0, -4.0, -6.0])


def pack_weight(w, fmt):
    k, n = w.shape
    w = f64(np.asarray(w, np.float32).astype(ml_dtypes.bfloat16)).reshape(k // 32, 32, n)
    amax = np.abs(w).max(1)
    if fmt == "e4m3":
        byte = np.frexp(amax)[1] - 1 + 127 - 7
    else:
        mant, ex = np.frexp(amax / 6.0)
        byte = np.where(mant > 0.5, ex, ex - 1) + 127
    byte = np.clip(np.where(amax > 0, byte, 1), 1, 254)
    scaled = (w * np.exp2(127.0 - byte)[:, None, :]).reshape(k, n).astype(np.float32)
    by_word = np.ascontiguousarray(scaled.reshape(k // 512, 128, 4, n).transpose(0, 1, 3, 2))
    if fmt == "e4m3":
        words = by_word.astype(ml_dtypes.float8_e4m3fn).view(np.uint8)
    else:
        c = by_word.astype(ml_dtypes.float4_e2m1fn).view(np.uint8) & 0xF
        words = (c[..., 0::2] | (c[..., 1::2] << 4)).reshape(k // 512, 128, 2 * n)
    return np.ascontiguousarray(words), np.ascontiguousarray(byte.astype(np.uint8).reshape(k // 512, 16, n))


def unpack_weight(words, scales, fmt):
    g, _, n = scales.shape
    words = np.ascontiguousarray(words).reshape(g, 128, n, -1)
    if fmt == "e4m3":
        vals = words.view(ml_dtypes.float8_e4m3fn).astype(np.float64)
    else:
        nib = np.empty((g, 128, n, 4), np.uint8)
        nib[..., 0::2] = words & 0xF
        nib[..., 1::2] = words >> 4
        vals = E2M1[nib]
    vals = vals * np.repeat(np.exp2(scales.astype(np.float64) - 127.0), 8, axis=1)[..., None]
    return vals.transpose(0, 1, 3, 2).reshape(g * 512, n)


def gelu(v):
    return 0.5 * v * (1.0 + np.tanh(np.sqrt(2.0 / np.pi) * (v + 0.044715 * v**3)))


K, T, S, H, N, T2 = 1024, 2048, 512, 1024, 512, 1024


def setup_inputs():
    n = np.random.standard_normal
    s = mx_kscale(K)[:, None]
    u = mx_kscale(H)[:, None]
    tab_words, tab_scales = pack_weight(n((K, T)) * s, "e4m3")
    wb_words, wb_scales = pack_weight(n((K, H)) / np.sqrt(K) / s, "e2m1")
    return {
        "tab_words": tab_words, "tab_scales": tab_scales,
        "offs": striped(np.random.permutation(T)[:S]),
        "offs2": striped(np.random.permutation(T)[:S]),
        "wa": (n((K, H)) / np.sqrt(K) / s).astype(np.float32),
        "wb_words": wb_words, "wb_scales": wb_scales,
        "gain": (np.random.uniform(0.5, 1.5, H) * u[:, 0]).astype(np.float32),
        "wc": (n((H, N)) / np.sqrt(H) / u).astype(np.float32),
        "stretch": np.random.uniform(0.5, 0.9, N).astype(np.float32),
        "wgo": np.exp(0.3 * n((128, S))).astype(np.float32),
        "offs3": striped(np.random.permutation(T2)[:S]),
    }


def reference(tab_words, tab_scales, offs, offs2, wa, wb_words, wb_scales, gain, wc, stretch, wgo, offs3):
    TW = unpack_weight(tab_words, tab_scales, "e4m3")
    v = TW[:, unstriped(offs)]
    v2 = TW[:, unstriped(offs2)]
    ment = mxq(f64(wa), 0, "e4m3").T @ v
    tor = unpack_weight(wb_words, wb_scales, "e2m1").T @ v2
    hi = np.maximum(ment, tor)
    lo = np.minimum(ment, tor)
    h = hi * np.tanh(lo) * f64(gain)[:, None]
    e = mxq(f64(wc), 0, "e4m3").T @ mxq(h, 0, "e4m3")
    y = np.sin(f64(stretch)[:, None] * e)
    out = np.zeros((N, T2))
    out[:, unstriped(offs3)] = np.tile(f64(wgo), (N // 128, 1)) * y
    return out

@@ -1,0 +1,308 @@
+import math
+from contextlib import ExitStack
+
+import concourse.mybir as mybir
+from concourse.masks import make_identity
+
+K, T, S, H, N, T2 = 1024, 2048, 512, 1024, 512, 1024
+FLOPS = 2 * S * (2 * K * H + H * N)
+
+F32 = mybir.dt.float32
+BF16 = mybir.dt.bfloat16
+I32 = mybir.dt.int32
+U32 = mybir.dt.uint32
+U16 = mybir.dt.uint16
+U8 = mybir.dt.uint8
+FP8X4 = mybir.dt.float8_e4m3fn_x4
+FP4X4 = mybir.dt.float4_e2m1fn_x4
+ALU = mybir.AluOpType
+ACT = mybir.ActivationFunctionType
+
+P = 128
+PACK = 4
+PASS = P * PACK
+KP = K // PASS
+HP = H // PASS
+NT = N // P
+HALF = S // 2
+RUN = 8
+ROUNDER = 1.5 * 2.0**23
+TINY = 2.0**-100
+
+
+def tile_list_mentoring_pair_proposals_kernel(
+    tc, tab_words, tab_scales, offs, offs2, wa, wb_words, wb_scales, gain, wc, stretch, wgo, offs3, out
+):
+    nc = tc.nc
+    with ExitStack() as ctx:
+        keep = ctx.enter_context(tc.tile_pool(name="keep", bufs=1))
+        ring = ctx.enter_context(tc.tile_pool(name="ring", bufs=3))
+        psum = ctx.enter_context(tc.psum_pool(name="psum", bufs=8))
+
+        def held(name, shape, dtype):
+            return keep.tile(shape, dtype, name=name, align_bytes=64)
+
+        def bank(name):
+            return psum.tile([P, S], F32, name=name, tag="bank")
+
+        idx = held("idx", [P, S // 16], U16)
+        idx2 = held("idx2", [P, S // 16], U16)
+        idx3 = held("idx3", [P, S // 16], U16)
+        tab_w = [held(f"tab_w{a}", [P, T], I32) for a in range(KP)]
+        tab_s = held("tab_s", [P, T // 4], I32)
+        wb_s_raw = held("wb_s_raw", [P, KP * H // 4], I32)
+        v2_s_last = held("v2_s_last", [P, S // 4], I32)
+        rows = held("rows", [P, HP * P], F32)
+        ident = held("ident", [P, P], F32)
+        pages = [held(f"page{nt}", [P, T2], F32) for nt in range(NT)]
+
+        nc.gpsimd.memset(tab_s[:], 0)
+        nc.vector.memset(rows[:], 0.0)
+        nc.vector.memset(wb_s_raw[:], 0)
+        nc.vector.memset(v2_s_last[:], 0)
+
+        def load_table(a):
+            nc.sync.dma_start(out=tab_w[a][:], in_=tab_words[a].rearrange("p t i -> p (t i)").bitcast(I32))
+
+        wa_raw = {}
+
+        def load_wa(a, b):
+            wa_raw[a, b] = held(f"wa_raw{a}{b}", [P, PACK, PASS], F32)
+            nc.sync.dma_start(
+                out=wa_raw[a, b][:],
+                in_=wa[a * PASS : (a + 1) * PASS, b * PASS : (b + 1) * PASS].rearrange("(p j) c -> p j c", j=PACK),
+            )
+
+        wb_raw = {}
+
+        def load_wb(b):
+            wb_raw[b] = held(f"wb_raw{b}", [P, KP, PASS // 2], I32)
+            nc.sync.dma_start(
+                out=wb_raw[b][:],
+                in_=wb_words.bitcast(I32)[:, :, b * (PASS // 2) : (b + 1) * (PASS // 2)].rearrange("a p w -> p a w"),
+            )
+
+        wc_raw = {}
+
+        def load_wc(b):
+            wc_raw[b] = held(f"wc_raw{b}", [P, PACK, N], F32)
+            by_slot = wc[b * PASS : (b + 1) * PASS, :].rearrange("(q t i) n -> t q i n", t=PACK, i=RUN)
+            for t in range(PACK):
+                nc.sync.dma_start(out=wc_raw[b][:, t, :], in_=by_slot[t])
+
+        nc.sync.dma_start(idx2[:], offs2)
+        nc.sync.dma_start(idx[:], offs)
+        load_table(0)
+        for q in range(4):
+            nc.scalar.dma_start(
+                out=tab_s[32 * q : 32 * q + 4 * KP, :], in_=tab_scales.bitcast(I32)[:, 4 * q : 4 * q + 4, :]
+            )
+        load_table(1)
+        v_s = held("v_s", [P, S], U8)
+        v2_s = held("v2_s", [P, S], U8)
+        nc.vector.tensor_copy(v2_s[:], tab_s[:].bitcast(U8).indirect(idx2[:]))
+        nc.scalar.dma_start(out=v2_s_last[0:100, :], in_=v2_s[4:104, :].bitcast(I32))
+        nc.gpsimd.dma_start(
+            out=rows[0:PACK, :].rearrange("t (g i) -> t g i", i=RUN),
+            in_=gain.rearrange("(g t i) -> t g i", t=PACK, i=RUN),
+        )
+        nc.gpsimd.dma_start(out=rows[PACK : PACK + NT, 0:P], in_=stretch.rearrange("(c p) -> c p", p=P))
+        load_wb(0)
+        for q in range(4):
+            nc.gpsimd.dma_start(
+                out=wb_s_raw[32 * q : 32 * q + 4, :].rearrange("r (a w) -> r a w", a=KP),
+                in_=wb_scales.bitcast(I32)[:, 4 * q : 4 * q + 4, :].rearrange("a r w -> r a w"),
+            )
+        make_identity(nc, ident[:])
+        load_wa(0, 0)
+        load_wa(1, 0)
+        load_wa(0, 1)
+        load_wb(1)
+        load_wa(1, 1)
+        load_wc(0)
+        load_wc(1)
+        wgo_sb = held("wgo_sb", [P, S], F32)
+        nc.sync.dma_start(out=wgo_sb[:], in_=wgo)
+        nc.sync.dma_start(idx3[:], offs3)
+
+        for page in pages:
+            nc.vector.memset(page[:], 0.0)
+
+        cols = bank("cols")
+        for b in range(HP):
+            nc.tensor.transpose(cols[:, b * P : (b + 1) * P], rows[:, b * P : (b + 1) * P], ident[:])
+        g_cols = cols[:, 0 : HP * P].rearrange("p (b c) -> p b c", b=HP)[:, :, 0:PACK]
+        g_abs = held("g_abs", [P, 8], F32)
+        g_sign = held("g_sign", [P, 8], F32)
+        turns = held("turns", [P, NT], F32)
+        g_mag = held("g_mag", [P, 8], F32)
+        g_rec = held("g_rec", [P, 8], F32)
+        g_inv = held("g_inv", [P, 8], F32)
+        nc.scalar.activation(g_abs[:].rearrange("p (b t) -> p b t", b=HP), g_cols, ACT.Abs)
+        nc.scalar.activation(g_sign[:].rearrange("p (b t) -> p b t", b=HP), g_cols, ACT.Sign)
+        nc.scalar.activation(turns[:], cols[:, PACK : PACK + NT], ACT.Copy, scale=1.0 / (2.0 * math.pi))
+        nc.vector.tensor_scalar_max(g_mag[:], g_abs[:], TINY)
+        nc.vector.reciprocal(g_rec[:], g_mag[:])
+        nc.vector.tensor_tensor(g_inv[:], g_rec[:], g_sign[:], ALU.mult)
+
+        v_w = [held(f"v_w{a}", [P, S], U32) for a in range(KP)]
+        v2_w = [held(f"v2_w{a}", [P, S], U32) for a in range(KP)]
+        nc.vector.tensor_copy(v_s[:], tab_s[:].bitcast(U8).indirect(idx[:]))
+        nc.vector.tensor_copy(v2_w[0][:], tab_w[0][:].bitcast(U32).indirect(idx2[:]))
+        nc.vector.tensor_copy(v_w[0][:], tab_w[0][:].bitcast(U32).indirect(idx[:]))
+        nc.vector.tensor_copy(v2_w[1][:], tab_w[1][:].bitcast(U32).indirect(idx2[:]))
+        nc.vector.tensor_copy(v_w[1][:], tab_w[1][:].bitcast(U32).indirect(idx[:]))
+        v2_planes = [v2_s[:], v2_s_last[:].bitcast(U8)]
+
+        wb_s = held("wb_s", [P, KP * H], U8)
+        nc.vector.tensor_copy(
+            out=wb_s[:].bitcast(I32).rearrange("p (g t q w) -> p g t q w", t=PACK, q=16, w=2),
+            in_=wb_s_raw[:].rearrange("p (g q t w) -> p g t q w", t=PACK, q=16, w=2),
+        )
+        wb_w = {}
+
+        def deal_wb(b):
+            wb_w[b] = held(f"wb_w{b}", [P, KP * 2 * PASS], U8)
+            nc.vector.tensor_copy(
+                out=wb_w[b][:].bitcast(I32).rearrange("p (a t q w) -> p a t q w", a=KP, t=PACK, w=4),
+                in_=wb_raw[b][:].rearrange("p a (q t w) -> p a t q w", t=PACK, w=4),
+            )
+
+        wa_bf, wa_w, wa_s = {}, {}, {}
+
+        def round_wa(a, b, t, copy):
+            if a == 0:
+                wa_bf[b, t] = held(f"wa_bf{b}{t}", [P, KP, PASS], BF16)
+            src = wa_raw[a, b][:].rearrange("p j (q t i e) -> p t q i j e", t=PACK, i=2, e=4)
+            copy(out=wa_bf[b, t][:, a, :].rearrange("p (q i e j) -> p q i j e", i=2, e=4, j=PACK), in_=src[:, t])
+
+        def quantize(name, src, width):
+            words = held(name + "_w", [P, width], U32)
+            scales = held(name + "_s", [P, width], U8)
+            nc.vector.quantize_mx(out=words[:].bitcast(FP8X4), scales=scales[:], in_=src)
+            return words, scales
+
+        def quantize_wa(b, t):
+            wa_w[b, t], wa_s[b, t] = quantize(f"wa{b}{t}", wa_bf[b, t][:].rearrange("p a c -> p (a c)"), KP * P)
+
+        wc_bf, wc_w, wc_s = {}, {}, {}
+
+        def round_wc(b, copy):
+            wc_bf[b] = held(f"wc_bf{b}", [P, N * PACK], BF16)
+            copy(
+                out=wc_bf[b][:].rearrange("p (c e t) -> p c t e", e=4, t=PACK),
+                in_=wc_raw[b][:].rearrange("p t (c e) -> p c t e", e=4),
+            )
+
+        def quantize_wc(b):
+            wc_w[b], wc_s[b] = quantize(f"wc{b}", wc_bf[b][:], N)
+
+        hi, th, h_w, h_s = {}, {}, {}, {}
+
+        def stage1(b, t):
+            if t == 0:
+                hi[b] = held(f"hi{b}", [P, PACK, S], F32)
+                th[b] = held(f"th{b}", [P, PACK, S], F32)
+            col = PACK * b + t
+            tor = bank(f"tor{col}")
+            for a in range(KP):
+                nc.tensor.matmul_mx(
+                    out=tor[:],
+                    lhsT=wb_w[b][:, (a * PACK + t) * 2 * P : (a * PACK + t + 1) * 2 * P].bitcast(FP4X4),
+                    lhsT_scale=wb_s[:, a * H + col * P : a * H + (col + 1) * P],
+                    rhs=v2_w[a][:].bitcast(FP8X4),
+                    rhs_scale=v2_planes[a],
+                    start=(a == 0),
+                    stop=(a == KP - 1),
+                )
+            tor_g = ring.tile([P, S], F32, name="tor_g", bufs=5)
+            nc.scalar.activation(tor_g[:], tor[:], ACT.Copy, scale=g_mag[:, col : col + 1])
+            ment = bank(f"ment{col}")
+            for a in range(KP):
+                nc.tensor.matmul_mx(
+                    out=ment[:],
+                    lhsT=wa_w[b, t][:, a * P : (a + 1) * P].bitcast(FP8X4),
+                    lhsT_scale=wa_s[b, t][:, a * P : (a + 1) * P],
+                    rhs=v_w[a][:].bitcast(FP8X4),
+                    rhs_scale=v_s[4 * a : P, :],
+                    start=(a == 0),
+                    stop=(a == KP - 1),
+                )
+            lo = ring.tile([P, S], F32, name="lo")
+            nc.vector.scalar_tensor_tensor(lo[:], ment[:], g_mag[:, col : col + 1], tor_g[:], ALU.mult, ALU.min)
+            nc.vector.scalar_tensor_tensor(hi[b][:, t, :], ment[:], g_mag[:, col : col + 1], tor_g[:], ALU.mult, ALU.max)
+            nc.scalar.activation(th[b][:, t, :], lo[:], ACT.Tanh, scale=g_inv[:, col : col + 1])
+
+        h_bf = {}
+
+        def join(b, half):
+            h_bf[b, half] = held(f"h_bf{b}{half}", [P, HALF * PACK], BF16)
+            entries = slice(half * HALF, (half + 1) * HALF)
+            nc.vector.tensor_tensor(
+                h_bf[b, half][:].rearrange("p (c e t) -> p c t e", e=4, t=PACK),
+                hi[b][:, :, entries].rearrange("p t (c e) -> p c t e", e=4),
+                th[b][:, :, entries].rearrange("p t (c e) -> p c t e", e=4),
+                ALU.mult,
+            )
+
+        def quantize_h(b, half):
+            h_w[b, half], h_s[b, half] = quantize(f"h{b}{half}", h_bf[b, half][:], HALF)
+
+        def stage2(half, nt):
+            e = bank(f"e{half}{nt}")
+            for b in range(HP):
+                nc.tensor.matmul_mx(
+                    out=e[:, 0:HALF],
+                    lhsT=wc_w[b][:, nt * P : (nt + 1) * P].bitcast(FP8X4),
+                    lhsT_scale=wc_s[b][:, nt * P : (nt + 1) * P],
+                    rhs=h_w[b, half][:].bitcast(FP8X4),
+                    rhs_scale=h_s[b, half][:],
+                    start=(b == 0),
+                    stop=(b == HP - 1),
+                )
+            shifted = ring.tile([P, HALF], U32, name="shifted")
+            whole = ring.tile([P, HALF], F32, name="whole")
+            frac = ring.tile([P, HALF], F32, name="frac")
+            y = ring.tile([P, HALF], F32, name="y")
+            nc.scalar.activation(shifted[:], e[:, 0:HALF], ACT.Copy, bias=ROUNDER, scale=turns[:, nt : nt + 1])
+            nc.scalar.activation(whole[:], shifted[:], ACT.Copy, bias=-ROUNDER)
+            nc.vector.scalar_tensor_tensor(frac[:], e[:, 0:HALF], turns[:, nt : nt + 1], whole[:], ALU.mult, ALU.subtract)
+            nc.scalar.activation(y[:], frac[:], ACT.Sin, scale=2.0 * math.pi)
+            places = idx3[:, half * (HALF // 16) : (half + 1) * (HALF // 16)]
+            nc.vector.tensor_tensor(
+                pages[nt][:].indirect(places), y[:], wgo_sb[:, half * HALF : (half + 1) * HALF], ALU.mult
+            )
+
+        def prepare(unit):
+            b, t = divmod(unit, PACK)
+            if t == 0:
+                deal_wb(b)
+            round_wa(0, b, t, nc.scalar.copy)
+            round_wa(1, b, t, nc.vector.tensor_copy if unit < 2 else nc.scalar.copy)
+            quantize_wa(b, t)
+
+        prepare(0)
+        for unit in range(HP * PACK):
+            if unit + 1 < HP * PACK:
+                prepare(unit + 1)
+            stage1(*divmod(unit, PACK))
+            if unit == 4:
+                join(0, 0)
+            if unit == 5:
+                quantize_h(0, 0)
+                join(0, 1)
+                round_wc(0, nc.scalar.copy)
+            if unit == 6:
+                quantize_h(0, 1)
+                quantize_wc(0)
+                round_wc(1, nc.scalar.copy)
+        quantize_wc(1)
+        join(1, 0)
+        quantize_h(1, 0)
+        join(1, 1)
+        quantize_h(1, 1)
+        for half in range(2):
+            for nt in range(NT):
+                stage2(half, nt)
+                if half == 1:
+                    nc.sync.dma_start(out=out[nt * P : (nt + 1) * P, :], in_=pages[nt][:])

@@ -53,6 +53,7 @@ def tile_list_mentoring_pair_proposals_kernel(
         wb_s_raw = held("wb_s_raw", [P, KP * H // 4], I32)
         v2_s_last = held("v2_s_last", [P, S // 4], I32)
         rows = held("rows", [P, HP * P], F32)
+        rows2 = held("rows2", [P, P], F32)
         ident = held("ident", [P, P], F32)
         pages = [held(f"page{nt}", [P, T2], F32) for nt in range(NT)]
 
@@ -60,6 +61,7 @@ def tile_list_mentoring_pair_proposals_kernel(
         nc.vector.memset(rows[:], 0.0)
         nc.vector.memset(wb_s_raw[:], 0)
         nc.vector.memset(v2_s_last[:], 0)
+        nc.vector.memset(rows2[:], 0.0)
 
         def load_table(a):
             nc.sync.dma_start(out=tab_w[a][:], in_=tab_words[a].rearrange("p t i -> p (t i)").bitcast(I32))
@@ -90,43 +92,45 @@ def tile_list_mentoring_pair_proposals_kernel(
             for t in range(PACK):
                 nc.sync.dma_start(out=wc_raw[b][:, t, :], in_=by_slot[t])
 
+        make_identity(nc, ident[:])
+        warm = held("warm", [P, 1], F32)
+        nc.scalar.activation(warm[:], ident[:, 0:1], ACT.Silu)
         nc.sync.dma_start(idx2[:], offs2)
         nc.sync.dma_start(idx[:], offs)
-        load_table(0)
         for q in range(4):
-            nc.scalar.dma_start(
+            nc.sync.dma_start(
                 out=tab_s[32 * q : 32 * q + 4 * KP, :], in_=tab_scales.bitcast(I32)[:, 4 * q : 4 * q + 4, :]
             )
+        load_table(0)
         load_table(1)
         v_s = held("v_s", [P, S], U8)
         v2_s = held("v2_s", [P, S], U8)
         nc.vector.tensor_copy(v2_s[:], tab_s[:].bitcast(U8).indirect(idx2[:]))
-        nc.scalar.dma_start(out=v2_s_last[0:100, :], in_=v2_s[4:104, :].bitcast(I32))
-        nc.gpsimd.dma_start(
+        nc.scalar.dma_start(out=v2_s_last[0:112, :], in_=v2_s[4:116, :].bitcast(I32))
+        nc.sync.dma_start(
             out=rows[0:PACK, :].rearrange("t (g i) -> t g i", i=RUN),
             in_=gain.rearrange("(g t i) -> t g i", t=PACK, i=RUN),
         )
-        nc.gpsimd.dma_start(out=rows[PACK : PACK + NT, 0:P], in_=stretch.rearrange("(c p) -> c p", p=P))
         load_wb(0)
         for q in range(4):
-            nc.gpsimd.dma_start(
+            nc.sync.dma_start(
                 out=wb_s_raw[32 * q : 32 * q + 4, :].rearrange("r (a w) -> r a w", a=KP),
                 in_=wb_scales.bitcast(I32)[:, 4 * q : 4 * q + 4, :].rearrange("a r w -> r a w"),
             )
-        make_identity(nc, ident[:])
         load_wa(0, 0)
         load_wa(1, 0)
         load_wa(0, 1)
         load_wb(1)
         load_wa(1, 1)
         load_wc(0)
+        nc.sync.dma_start(out=rows2[0:NT, :], in_=stretch.rearrange("(c p) -> c p", p=P))
         load_wc(1)
         wgo_sb = held("wgo_sb", [P, S], F32)
         nc.sync.dma_start(out=wgo_sb[:], in_=wgo)
         nc.sync.dma_start(idx3[:], offs3)
 
-        for page in pages:
-            nc.vector.memset(page[:], 0.0)
+        for nt, page in enumerate(pages):
+            (nc.vector if nt < 2 else nc.gpsimd).memset(page[:], 0.0)
 
         cols = bank("cols")
         for b in range(HP):
@@ -140,7 +144,6 @@ def tile_list_mentoring_pair_proposals_kernel(
         g_inv = held("g_inv", [P, 8], F32)
         nc.scalar.activation(g_abs[:].rearrange("p (b t) -> p b t", b=HP), g_cols, ACT.Abs)
         nc.scalar.activation(g_sign[:].rearrange("p (b t) -> p b t", b=HP), g_cols, ACT.Sign)
-        nc.scalar.activation(turns[:], cols[:, PACK : PACK + NT], ACT.Copy, scale=1.0 / (2.0 * math.pi))
         nc.vector.tensor_scalar_max(g_mag[:], g_abs[:], TINY)
         nc.vector.reciprocal(g_rec[:], g_mag[:])
         nc.vector.tensor_tensor(g_inv[:], g_rec[:], g_sign[:], ALU.mult)
@@ -277,8 +280,8 @@ def tile_list_mentoring_pair_proposals_kernel(
             b, t = divmod(unit, PACK)
             if t == 0:
                 deal_wb(b)
-            round_wa(0, b, t, nc.scalar.copy)
-            round_wa(1, b, t, nc.vector.tensor_copy if unit < 2 else nc.scalar.copy)
+            round_wa(0, b, t, nc.vector.tensor_copy if b == 0 else nc.scalar.copy)
+            round_wa(1, b, t, nc.vector.tensor_copy if unit == 0 else nc.scalar.copy)
             quantize_wa(b, t)
 
         prepare(0)
@@ -296,6 +299,9 @@ def tile_list_mentoring_pair_proposals_kernel(
                 quantize_h(0, 1)
                 quantize_wc(0)
                 round_wc(1, nc.scalar.copy)
+        cols2 = bank("cols2")
+        nc.tensor.transpose(cols2[:, 0:P], rows2[:], ident[:])
+        nc.scalar.activation(turns[:], cols2[:, 0:NT], ACT.Copy, scale=1.0 / (2.0 * math.pi))
         quantize_wc(1)
         join(1, 0)
         quantize_h(1, 0)

@@ -171,34 +171,44 @@ def tile_list_mentoring_pair_proposals_kernel(
                 in_=wb_raw[b][:].rearrange("p a (q t w) -> p a t q w", t=PACK, w=4),
             )
 
-        wa_bf, wa_w, wa_s = {}, {}, {}
-
-        def round_wa(a, b, t, copy):
-            if a == 0:
-                wa_bf[b, t] = held(f"wa_bf{b}{t}", [P, KP, PASS], BF16)
-            src = wa_raw[a, b][:].rearrange("p j (q t i e) -> p t q i j e", t=PACK, i=2, e=4)
-            copy(out=wa_bf[b, t][:, a, :].rearrange("p (q i e j) -> p q i j e", i=2, e=4, j=PACK), in_=src[:, t])
-
         def quantize(name, src, width):
             words = held(name + "_w", [P, width], U32)
             scales = held(name + "_s", [P, width], U8)
             nc.vector.quantize_mx(out=words[:].bitcast(FP8X4), scales=scales[:], in_=src)
             return words, scales
 
-        def quantize_wa(b, t):
-            wa_w[b, t], wa_s[b, t] = quantize(f"wa{b}{t}", wa_bf[b, t][:].rearrange("p a c -> p (a c)"), KP * P)
+        wa_w, wa_s = {}, {}
+
+        def round_wa(a, b, t, dst, copy):
+            src = wa_raw[a, b][:].rearrange("p j (q t i e) -> p t q i j e", t=PACK, i=2, e=4)
+            copy(out=dst.rearrange("p (q i e j) -> p q i j e", i=2, e=4, j=PACK), in_=src[:, t])
+
+        def prepare_first_pass(b, copy):
+            rounded = held(f"wa_bf0{b}", [P, PACK * PASS], BF16)
+            for t in range(PACK):
+                round_wa(0, b, t, rounded[:, t * PASS : (t + 1) * PASS], copy)
+            words, scales = quantize(f"wa0{b}", rounded[:], PASS)
+            for t in range(PACK):
+                wa_w[0, b, t], wa_s[0, b, t] = words[:, t * P : (t + 1) * P], scales[:, t * P : (t + 1) * P]
+
+        def prepare_second_pass(b, t, copy):
+            rounded = held(f"wa_bf1{b}{t}", [P, PASS], BF16)
+            round_wa(1, b, t, rounded[:], copy)
+            words, scales = quantize(f"wa1{b}{t}", rounded[:], P)
+            wa_w[1, b, t], wa_s[1, b, t] = words[:], scales[:]
 
         wc_bf, wc_w, wc_s = {}, {}, {}
 
-        def round_wc(b, copy):
-            wc_bf[b] = held(f"wc_bf{b}", [P, N * PACK], BF16)
-            copy(
-                out=wc_bf[b][:].rearrange("p (c e t) -> p c t e", e=4, t=PACK),
-                in_=wc_raw[b][:].rearrange("p t (c e) -> p c t e", e=4),
-            )
+        def round_wc(nt):
+            wc_bf[nt] = held(f"wc_bf{nt}", [P, HP, PASS], BF16)
+            for b in range(HP):
+                nc.scalar.copy(
+                    out=wc_bf[nt][:, b, :].rearrange("p (c e t) -> p c t e", e=4, t=PACK),
+                    in_=wc_raw[b][:, :, nt * P : (nt + 1) * P].rearrange("p t (c e) -> p c t e", e=4),
+                )
 
-        def quantize_wc(b):
-            wc_w[b], wc_s[b] = quantize(f"wc{b}", wc_bf[b][:], N)
+        def quantize_wc(nt):
+            wc_w[nt], wc_s[nt] = quantize(f"wc{nt}", wc_bf[nt][:].rearrange("p b c -> p (b c)"), HP * P)
 
         hi, th, h_w, h_s = {}, {}, {}, {}
 
@@ -224,8 +234,8 @@ def tile_list_mentoring_pair_proposals_kernel(
             for a in range(KP):
                 nc.tensor.matmul_mx(
                     out=ment[:],
-                    lhsT=wa_w[b, t][:, a * P : (a + 1) * P].bitcast(FP8X4),
-                    lhsT_scale=wa_s[b, t][:, a * P : (a + 1) * P],
+                    lhsT=wa_w[a, b, t].bitcast(FP8X4),
+                    lhsT_scale=wa_s[a, b, t],
                     rhs=v_w[a][:].bitcast(FP8X4),
                     rhs_scale=v_s[4 * a : P, :],
                     start=(a == 0),
@@ -242,22 +252,24 @@ def tile_list_mentoring_pair_proposals_kernel(
             h_bf[b, half] = held(f"h_bf{b}{half}", [P, HALF * PACK], BF16)
             entries = slice(half * HALF, (half + 1) * HALF)
             nc.vector.tensor_tensor(
-                h_bf[b, half][:].rearrange("p (c e t) -> p c t e", e=4, t=PACK),
-                hi[b][:, :, entries].rearrange("p t (c e) -> p c t e", e=4),
-                th[b][:, :, entries].rearrange("p t (c e) -> p c t e", e=4),
+                h_bf[b, half][:].rearrange("p (c e t) -> p c t e", e=2, t=PACK),
+                hi[b][:, :, entries].rearrange("p t (c e) -> p c t e", e=2),
+                th[b][:, :, entries].rearrange("p t (c e) -> p c t e", e=2),
                 ALU.mult,
             )
 
         def quantize_h(b, half):
             h_w[b, half], h_s[b, half] = quantize(f"h{b}{half}", h_bf[b, half][:], HALF)
 
+        frac = {}
+
         def stage2(half, nt):
             e = bank(f"e{half}{nt}")
             for b in range(HP):
                 nc.tensor.matmul_mx(
                     out=e[:, 0:HALF],
-                    lhsT=wc_w[b][:, nt * P : (nt + 1) * P].bitcast(FP8X4),
-                    lhsT_scale=wc_s[b][:, nt * P : (nt + 1) * P],
+                    lhsT=wc_w[nt][:, b * P : (b + 1) * P].bitcast(FP8X4),
+                    lhsT_scale=wc_s[nt][:, b * P : (b + 1) * P],
                     rhs=h_w[b, half][:].bitcast(FP8X4),
                     rhs_scale=h_s[b, half][:],
                     start=(b == 0),
@@ -265,12 +277,14 @@ def tile_list_mentoring_pair_proposals_kernel(
                 )
             shifted = ring.tile([P, HALF], U32, name="shifted")
             whole = ring.tile([P, HALF], F32, name="whole")
-            frac = ring.tile([P, HALF], F32, name="frac")
-            y = ring.tile([P, HALF], F32, name="y")
+            frac[half, nt] = ring.tile([P, HALF], F32, name="frac")
             nc.scalar.activation(shifted[:], e[:, 0:HALF], ACT.Copy, bias=ROUNDER, scale=turns[:, nt : nt + 1])
             nc.scalar.activation(whole[:], shifted[:], ACT.Copy, bias=-ROUNDER)
-            nc.vector.scalar_tensor_tensor(frac[:], e[:, 0:HALF], turns[:, nt : nt + 1], whole[:], ALU.mult, ALU.subtract)
-            nc.scalar.activation(y[:], frac[:], ACT.Sin, scale=2.0 * math.pi)
+            nc.vector.scalar_tensor_tensor(frac[half, nt][:], e[:, 0:HALF], turns[:, nt : nt + 1], whole[:], ALU.mult, ALU.subtract)
+
+        def place(half, nt):
+            y = ring.tile([P, HALF], F32, name="y")
+            nc.scalar.activation(y[:], frac[half, nt][:], ACT.Sin, scale=2.0 * math.pi)
             places = idx3[:, half * (HALF // 16) : (half + 1) * (HALF // 16)]
             nc.vector.tensor_tensor(
                 pages[nt][:].indirect(places), y[:], wgo_sb[:, half * HALF : (half + 1) * HALF], ALU.mult
@@ -280,9 +294,8 @@ def tile_list_mentoring_pair_proposals_kernel(
             b, t = divmod(unit, PACK)
             if t == 0:
                 deal_wb(b)
-            round_wa(0, b, t, nc.vector.tensor_copy if b == 0 else nc.scalar.copy)
-            round_wa(1, b, t, nc.vector.tensor_copy if unit == 0 else nc.scalar.copy)
-            quantize_wa(b, t)
+                prepare_first_pass(b, nc.vector.tensor_copy if b == 0 else nc.scalar.copy)
+            prepare_second_pass(b, t, nc.vector.tensor_copy if unit == 0 else nc.scalar.copy)
 
         prepare(0)
         for unit in range(HP * PACK):
@@ -294,21 +307,27 @@ def tile_list_mentoring_pair_proposals_kernel(
             if unit == 5:
                 quantize_h(0, 0)
                 join(0, 1)
-                round_wc(0, nc.scalar.copy)
             if unit == 6:
                 quantize_h(0, 1)
-                quantize_wc(0)
-                round_wc(1, nc.scalar.copy)
+                round_wc(0)
         cols2 = bank("cols2")
         nc.tensor.transpose(cols2[:, 0:P], rows2[:], ident[:])
         nc.scalar.activation(turns[:], cols2[:, 0:NT], ACT.Copy, scale=1.0 / (2.0 * math.pi))
-        quantize_wc(1)
+        quantize_wc(0)
+        round_wc(1)
         join(1, 0)
+        quantize_wc(1)
         quantize_h(1, 0)
         join(1, 1)
+        pieces = [(half, nt) for half in range(2) for nt in range(NT)]
+        stage2(*pieces[0])
         quantize_h(1, 1)
-        for half in range(2):
-            for nt in range(NT):
-                stage2(half, nt)
-                if half == 1:
-                    nc.sync.dma_start(out=out[nt * P : (nt + 1) * P, :], in_=pages[nt][:])
+        for n, (half, nt) in enumerate(pieces):
+            if n + 2 < NT:
+                round_wc(n + 2)
+                quantize_wc(n + 2)
+            if n + 1 < len(pieces):
+                stage2(*pieces[n + 1])
+            place(half, nt)
+            if half == 1:
+                nc.sync.dma_start(out=out[nt * P : (nt + 1) * P, :], in_=pages[nt][:])

@@ -21,11 +21,19 @@ ACT = mybir.ActivationFunctionType
 P = 128
 PACK = 4
 PASS = P * PACK
-KP = K // PASS
-HP = H // PASS
-NT = N // P
+K_PASSES = K // PASS
+R_PASSES = H // PASS
+SLOTS = R_PASSES * PACK
+N_TILES = N // P
 HALF = S // 2
 RUN = 8
+BLOCKS = PASS // 32
+QUADRANTS = 4
+SCALE_ROWS = 4
+LIST_ROWS = 16
+LAST_SCALE_ROW = 32 * (QUADRANTS - 1) + SCALE_ROWS
+VECTOR_PAGES = 2
+TOR_BUFS = PACK + 1
 ROUNDER = 1.5 * 2.0**23
 TINY = 2.0**-100
 
@@ -39,34 +47,39 @@ def tile_list_mentoring_pair_proposals_kernel(
         ring = ctx.enter_context(tc.tile_pool(name="ring", bufs=3))
         psum = ctx.enter_context(tc.psum_pool(name="psum", bufs=8))
 
-        def held(name, shape, dtype):
-            return keep.tile(shape, dtype, name=name, align_bytes=64)
+        def held(name, shape, dtype, tag=""):
+            return keep.tile(shape, dtype, name=name, tag=tag or name, align_bytes=64)
 
         def bank(name):
             return psum.tile([P, S], F32, name=name, tag="bank")
 
-        idx = held("idx", [P, S // 16], U16)
-        idx2 = held("idx2", [P, S // 16], U16)
-        idx3 = held("idx3", [P, S // 16], U16)
-        tab_w = [held(f"tab_w{a}", [P, T], I32) for a in range(KP)]
+        idx = held("idx", [P, S // LIST_ROWS], U16)
+        idx2 = held("idx2", [P, S // LIST_ROWS], U16)
+        idx3 = held("idx3", [P, S // LIST_ROWS], U16)
+        tab_w = [held(f"tab_w{a}", [P, T], I32) for a in range(K_PASSES)]
         tab_s = held("tab_s", [P, T // 4], I32)
-        wb_s_raw = held("wb_s_raw", [P, KP * H // 4], I32)
+        wb_s_raw = held("wb_s_raw", [P, K_PASSES * H // 4], I32)
         v2_s_last = held("v2_s_last", [P, S // 4], I32)
-        rows = held("rows", [P, HP * P], F32)
-        rows2 = held("rows2", [P, P], F32)
+        gain_rows = held("gain_rows", [R_PASSES, PASS], F32)
+        rows = held("rows", [P, PACK * P], F32)
         ident = held("ident", [P, P], F32)
-        pages = [held(f"page{nt}", [P, T2], F32) for nt in range(NT)]
+        pages = [held(f"page{nt}", [P, T2], F32) for nt in range(N_TILES)]
 
         nc.gpsimd.memset(tab_s[:], 0)
-        nc.vector.memset(rows[:], 0.0)
+        make_identity(nc, ident[:])
         nc.vector.memset(wb_s_raw[:], 0)
+        nc.vector.memset(rows[:], 0.0)
         nc.vector.memset(v2_s_last[:], 0)
-        nc.vector.memset(rows2[:], 0.0)
+        for nt, page in enumerate(pages):
+            (nc.vector if nt < VECTOR_PAGES else nc.gpsimd).memset(page[:], 0.0)
+
+        warm = held("warm", [P, 1], F32)
+        nc.scalar.activation(warm[:], ident[:, 0:1], ACT.Silu)
+
+        wa_raw, wb_raw, wc_raw = {}, {}, {}
 
         def load_table(a):
             nc.sync.dma_start(out=tab_w[a][:], in_=tab_words[a].rearrange("p t i -> p (t i)").bitcast(I32))
-
-        wa_raw = {}
 
         def load_wa(a, b):
             wa_raw[a, b] = held(f"wa_raw{a}{b}", [P, PACK, PASS], F32)
@@ -75,100 +88,96 @@ def tile_list_mentoring_pair_proposals_kernel(
                 in_=wa[a * PASS : (a + 1) * PASS, b * PASS : (b + 1) * PASS].rearrange("(p j) c -> p j c", j=PACK),
             )
 
-        wb_raw = {}
-
         def load_wb(b):
-            wb_raw[b] = held(f"wb_raw{b}", [P, KP, PASS // 2], I32)
+            wb_raw[b] = held(f"wb_raw{b}", [P, K_PASSES, PASS // 2], I32)
             nc.sync.dma_start(
                 out=wb_raw[b][:],
                 in_=wb_words.bitcast(I32)[:, :, b * (PASS // 2) : (b + 1) * (PASS // 2)].rearrange("a p w -> p a w"),
             )
 
-        wc_raw = {}
-
         def load_wc(b):
             wc_raw[b] = held(f"wc_raw{b}", [P, PACK, N], F32)
-            by_slot = wc[b * PASS : (b + 1) * PASS, :].rearrange("(q t i) n -> t q i n", t=PACK, i=RUN)
+            by_code = wc[b * PASS : (b + 1) * PASS, :].rearrange("(q t i) n -> t q i n", t=PACK, i=RUN)
             for t in range(PACK):
-                nc.sync.dma_start(out=wc_raw[b][:, t, :], in_=by_slot[t])
+                nc.sync.dma_start(out=wc_raw[b][:, t, :], in_=by_code[t])
 
-        make_identity(nc, ident[:])
-        warm = held("warm", [P, 1], F32)
-        nc.scalar.activation(warm[:], ident[:, 0:1], ACT.Silu)
         nc.sync.dma_start(idx2[:], offs2)
         nc.sync.dma_start(idx[:], offs)
-        for q in range(4):
+        for quad in range(QUADRANTS):
             nc.sync.dma_start(
-                out=tab_s[32 * q : 32 * q + 4 * KP, :], in_=tab_scales.bitcast(I32)[:, 4 * q : 4 * q + 4, :]
+                out=tab_s[32 * quad : 32 * quad + SCALE_ROWS * K_PASSES, :],
+                in_=tab_scales.bitcast(I32)[:, SCALE_ROWS * quad : SCALE_ROWS * (quad + 1), :],
             )
         load_table(0)
         load_table(1)
         v_s = held("v_s", [P, S], U8)
         v2_s = held("v2_s", [P, S], U8)
         nc.vector.tensor_copy(v2_s[:], tab_s[:].bitcast(U8).indirect(idx2[:]))
-        nc.scalar.dma_start(out=v2_s_last[0:112, :], in_=v2_s[4:116, :].bitcast(I32))
-        nc.sync.dma_start(
-            out=rows[0:PACK, :].rearrange("t (g i) -> t g i", i=RUN),
-            in_=gain.rearrange("(g t i) -> t g i", t=PACK, i=RUN),
+        nc.scalar.dma_start(
+            out=v2_s_last[0:LAST_SCALE_ROW, :], in_=v2_s[SCALE_ROWS : SCALE_ROWS + LAST_SCALE_ROW, :].bitcast(I32)
         )
+        nc.sync.dma_start(out=gain_rows[:], in_=gain.rearrange("(b c) -> b c", b=R_PASSES))
         load_wb(0)
-        for q in range(4):
+        for quad in range(QUADRANTS):
             nc.sync.dma_start(
-                out=wb_s_raw[32 * q : 32 * q + 4, :].rearrange("r (a w) -> r a w", a=KP),
-                in_=wb_scales.bitcast(I32)[:, 4 * q : 4 * q + 4, :].rearrange("a r w -> r a w"),
+                out=wb_s_raw[32 * quad : 32 * quad + SCALE_ROWS, :].rearrange("r (a w) -> r a w", a=K_PASSES),
+                in_=wb_scales.bitcast(I32)[:, SCALE_ROWS * quad : SCALE_ROWS * (quad + 1), :].rearrange("a r w -> r a w"),
             )
         load_wa(0, 0)
         load_wa(1, 0)
-        load_wa(0, 1)
         load_wb(1)
+        load_wa(0, 1)
         load_wa(1, 1)
         load_wc(0)
-        nc.sync.dma_start(out=rows2[0:NT, :], in_=stretch.rearrange("(c p) -> c p", p=P))
         load_wc(1)
         wgo_sb = held("wgo_sb", [P, S], F32)
         nc.sync.dma_start(out=wgo_sb[:], in_=wgo)
         nc.sync.dma_start(idx3[:], offs3)
 
-        for nt, page in enumerate(pages):
-            (nc.vector if nt < 2 else nc.gpsimd).memset(page[:], 0.0)
-
-        cols = bank("cols")
-        for b in range(HP):
-            nc.tensor.transpose(cols[:, b * P : (b + 1) * P], rows[:, b * P : (b + 1) * P], ident[:])
-        g_cols = cols[:, 0 : HP * P].rearrange("p (b c) -> p b c", b=HP)[:, :, 0:PACK]
-        g_abs = held("g_abs", [P, 8], F32)
-        g_sign = held("g_sign", [P, 8], F32)
-        turns = held("turns", [P, NT], F32)
-        g_mag = held("g_mag", [P, 8], F32)
-        g_rec = held("g_rec", [P, 8], F32)
-        g_inv = held("g_inv", [P, 8], F32)
-        nc.scalar.activation(g_abs[:].rearrange("p (b t) -> p b t", b=HP), g_cols, ACT.Abs)
-        nc.scalar.activation(g_sign[:].rearrange("p (b t) -> p b t", b=HP), g_cols, ACT.Sign)
-        nc.vector.tensor_scalar_max(g_mag[:], g_abs[:], TINY)
+        gain_bank = bank("gain_bank")
+        nc.scalar.copy(
+            out=rows[0:R_PASSES, :].rearrange("b (t q i) -> b t q i", t=PACK, i=RUN),
+            in_=gain_rows[:].rearrange("b (q t i) -> b t q i", t=PACK, i=RUN),
+        )
+        for t in range(PACK):
+            nc.tensor.transpose(gain_bank[:, t * P : (t + 1) * P], rows[:, t * P : (t + 1) * P], ident[:])
+        g_cols = gain_bank[:].rearrange("p (t c) -> p c t", t=PACK)[:, 0:R_PASSES, :]
+        nc.sync.dma_start(out=rows[R_PASSES : R_PASSES + N_TILES, 0:P], in_=stretch.rearrange("(c p) -> c p", p=P))
+        g_abs = held("g_abs", [P, SLOTS], F32)
+        g_sign = held("g_sign", [P, SLOTS], F32)
+        turns = held("turns", [P, N_TILES], F32)
+        g_mag = held("g_mag", [P, SLOTS], F32)
+        g_rec = held("g_rec", [P, SLOTS], F32)
+        g_inv = held("g_inv", [P, SLOTS], F32)
+        nc.scalar.activation(g_abs[:].rearrange("p (b t) -> p b t", b=R_PASSES), g_cols, ACT.Abs)
+        nc.scalar.activation(g_sign[:].rearrange("p (b t) -> p b t", b=R_PASSES), g_cols, ACT.Sign)
+        nc.scalar.activation(g_mag[:], g_abs[:], ACT.Copy, bias=TINY)
         nc.vector.reciprocal(g_rec[:], g_mag[:])
         nc.vector.tensor_tensor(g_inv[:], g_rec[:], g_sign[:], ALU.mult)
 
-        v_w = [held(f"v_w{a}", [P, S], U32) for a in range(KP)]
-        v2_w = [held(f"v2_w{a}", [P, S], U32) for a in range(KP)]
+        v_w = [held("v_w0", [P, S], U32)]
+        v2_w = [held(f"v2_w{a}", [P, S], U32) for a in range(K_PASSES)]
         nc.vector.tensor_copy(v_s[:], tab_s[:].bitcast(U8).indirect(idx[:]))
         nc.vector.tensor_copy(v2_w[0][:], tab_w[0][:].bitcast(U32).indirect(idx2[:]))
         nc.vector.tensor_copy(v_w[0][:], tab_w[0][:].bitcast(U32).indirect(idx[:]))
         nc.vector.tensor_copy(v2_w[1][:], tab_w[1][:].bitcast(U32).indirect(idx2[:]))
-        nc.vector.tensor_copy(v_w[1][:], tab_w[1][:].bitcast(U32).indirect(idx[:]))
-        v2_planes = [v2_s[:], v2_s_last[:].bitcast(U8)]
+        v2_scales = [v2_s[:], v2_s_last[:].bitcast(U8)]
 
-        wb_s = held("wb_s", [P, KP * H], U8)
+        wb_s = held("wb_s", [P, K_PASSES * H], U8)
         nc.vector.tensor_copy(
-            out=wb_s[:].bitcast(I32).rearrange("p (g t q w) -> p g t q w", t=PACK, q=16, w=2),
-            in_=wb_s_raw[:].rearrange("p (g q t w) -> p g t q w", t=PACK, q=16, w=2),
+            out=wb_s[:].bitcast(I32).rearrange("p (g t q w) -> p g t q w", t=PACK, q=BLOCKS, w=RUN // 4),
+            in_=wb_s_raw[:].rearrange("p (g q t w) -> p g t q w", t=PACK, q=BLOCKS, w=RUN // 4),
         )
-        wb_w = {}
+        v_w.append(held("v_w1", [P, S], U32, tag="wb_s_raw"))
+        nc.vector.tensor_copy(v_w[1][:], tab_w[1][:].bitcast(U32).indirect(idx[:]))
+
+        wb_w, wa_bf, wa_w, wa_s, wc_bf, wc_w, wc_s = {}, {}, {}, {}, {}, {}, {}
 
         def deal_wb(b):
-            wb_w[b] = held(f"wb_w{b}", [P, KP * 2 * PASS], U8)
+            wb_w[b] = held(f"wb_w{b}", [P, K_PASSES * 2 * PASS], U8)
             nc.vector.tensor_copy(
-                out=wb_w[b][:].bitcast(I32).rearrange("p (a t q w) -> p a t q w", a=KP, t=PACK, w=4),
-                in_=wb_raw[b][:].rearrange("p a (q t w) -> p a t q w", t=PACK, w=4),
+                out=wb_w[b][:].bitcast(I32).rearrange("p (a t q w) -> p a t q w", a=K_PASSES, t=PACK, w=RUN // 2),
+                in_=wb_raw[b][:].rearrange("p a (q t w) -> p a t q w", t=PACK, w=RUN // 2),
             )
 
         def quantize(name, src, width):
@@ -177,76 +186,70 @@ def tile_list_mentoring_pair_proposals_kernel(
             nc.vector.quantize_mx(out=words[:].bitcast(FP8X4), scales=scales[:], in_=src)
             return words, scales
 
-        wa_w, wa_s = {}, {}
+        def round_wa(a, b, t, copy):
+            wa_bf[a, b, t] = held(f"wa_bf{a}{b}{t}", [P, PASS], BF16)
+            src = wa_raw[a, b][:].rearrange("p j (q t u e) -> p t q u j e", t=PACK, u=RUN // 4, e=4)
+            copy(out=wa_bf[a, b, t][:].rearrange("p (q u e j) -> p q u j e", u=RUN // 4, e=4, j=PACK), in_=src[:, t])
 
-        def round_wa(a, b, t, dst, copy):
-            src = wa_raw[a, b][:].rearrange("p j (q t i e) -> p t q i j e", t=PACK, i=2, e=4)
-            copy(out=dst.rearrange("p (q i e j) -> p q i j e", i=2, e=4, j=PACK), in_=src[:, t])
+        def quantize_wa(a, b, t):
+            wa_w[a, b, t], wa_s[a, b, t] = quantize(f"wa{a}{b}{t}", wa_bf[a, b, t][:], P)
 
-        def prepare_first_pass(b, copy):
-            rounded = held(f"wa_bf0{b}", [P, PACK * PASS], BF16)
-            for t in range(PACK):
-                round_wa(0, b, t, rounded[:, t * PASS : (t + 1) * PASS], copy)
-            words, scales = quantize(f"wa0{b}", rounded[:], PASS)
-            for t in range(PACK):
-                wa_w[0, b, t], wa_s[0, b, t] = words[:, t * P : (t + 1) * P], scales[:, t * P : (t + 1) * P]
-
-        def prepare_second_pass(b, t, copy):
-            rounded = held(f"wa_bf1{b}{t}", [P, PASS], BF16)
-            round_wa(1, b, t, rounded[:], copy)
-            words, scales = quantize(f"wa1{b}{t}", rounded[:], P)
-            wa_w[1, b, t], wa_s[1, b, t] = words[:], scales[:]
-
-        wc_bf, wc_w, wc_s = {}, {}, {}
+        def prepare(slot):
+            b, t = divmod(slot, PACK)
+            if t == 0:
+                deal_wb(b)
+            round_wa(0, b, t, nc.vector.tensor_copy if b == 0 else nc.scalar.copy)
+            round_wa(1, b, t, nc.vector.tensor_copy if slot == 0 else nc.scalar.copy)
+            for a in range(K_PASSES):
+                quantize_wa(a, b, t)
 
         def round_wc(nt):
-            wc_bf[nt] = held(f"wc_bf{nt}", [P, HP, PASS], BF16)
-            for b in range(HP):
+            wc_bf[nt] = held(f"wc_bf{nt}", [P, R_PASSES, PASS], BF16)
+            for b in range(R_PASSES):
                 nc.scalar.copy(
                     out=wc_bf[nt][:, b, :].rearrange("p (c e t) -> p c t e", e=4, t=PACK),
                     in_=wc_raw[b][:, :, nt * P : (nt + 1) * P].rearrange("p t (c e) -> p c t e", e=4),
                 )
 
         def quantize_wc(nt):
-            wc_w[nt], wc_s[nt] = quantize(f"wc{nt}", wc_bf[nt][:].rearrange("p b c -> p (b c)"), HP * P)
+            wc_w[nt], wc_s[nt] = quantize(f"wc{nt}", wc_bf[nt][:].rearrange("p b c -> p (b c)"), R_PASSES * P)
 
-        hi, th, h_w, h_s = {}, {}, {}, {}
+        hi, th, h_bf, h_w, h_s = {}, {}, {}, {}, {}
 
-        def stage1(b, t):
+        def first_products(slot):
+            b, t = divmod(slot, PACK)
             if t == 0:
                 hi[b] = held(f"hi{b}", [P, PACK, S], F32)
                 th[b] = held(f"th{b}", [P, PACK, S], F32)
-            col = PACK * b + t
-            tor = bank(f"tor{col}")
-            for a in range(KP):
+            mag = g_mag[:, slot : slot + 1]
+            tor = bank(f"tor{slot}")
+            for a in range(K_PASSES):
                 nc.tensor.matmul_mx(
                     out=tor[:],
                     lhsT=wb_w[b][:, (a * PACK + t) * 2 * P : (a * PACK + t + 1) * 2 * P].bitcast(FP4X4),
-                    lhsT_scale=wb_s[:, a * H + col * P : a * H + (col + 1) * P],
+                    lhsT_scale=wb_s[:, a * H + slot * P : a * H + (slot + 1) * P],
                     rhs=v2_w[a][:].bitcast(FP8X4),
-                    rhs_scale=v2_planes[a],
+                    rhs_scale=v2_scales[a],
                     start=(a == 0),
-                    stop=(a == KP - 1),
+                    stop=(a == K_PASSES - 1),
                 )
-            tor_g = ring.tile([P, S], F32, name="tor_g", bufs=5)
-            nc.scalar.activation(tor_g[:], tor[:], ACT.Copy, scale=g_mag[:, col : col + 1])
-            ment = bank(f"ment{col}")
-            for a in range(KP):
+            tor_g = ring.tile([P, S], F32, name="tor_g", bufs=TOR_BUFS)
+            nc.scalar.activation(tor_g[:], tor[:], ACT.Copy, scale=mag)
+            ment = bank(f"ment{slot}")
+            for a in range(K_PASSES):
                 nc.tensor.matmul_mx(
                     out=ment[:],
-                    lhsT=wa_w[a, b, t].bitcast(FP8X4),
-                    lhsT_scale=wa_s[a, b, t],
+                    lhsT=wa_w[a, b, t][:].bitcast(FP8X4),
+                    lhsT_scale=wa_s[a, b, t][:],
                     rhs=v_w[a][:].bitcast(FP8X4),
-                    rhs_scale=v_s[4 * a : P, :],
+                    rhs_scale=v_s[SCALE_ROWS * a : P, :],
                     start=(a == 0),
-                    stop=(a == KP - 1),
+                    stop=(a == K_PASSES - 1),
                 )
             lo = ring.tile([P, S], F32, name="lo")
-            nc.vector.scalar_tensor_tensor(lo[:], ment[:], g_mag[:, col : col + 1], tor_g[:], ALU.mult, ALU.min)
-            nc.vector.scalar_tensor_tensor(hi[b][:, t, :], ment[:], g_mag[:, col : col + 1], tor_g[:], ALU.mult, ALU.max)
-            nc.scalar.activation(th[b][:, t, :], lo[:], ACT.Tanh, scale=g_inv[:, col : col + 1])
-
-        h_bf = {}
+            nc.vector.scalar_tensor_tensor(lo[:], ment[:], mag, tor_g[:], ALU.mult, ALU.min)
+            nc.vector.scalar_tensor_tensor(hi[b][:, t, :], ment[:], mag, tor_g[:], ALU.mult, ALU.max)
+            nc.scalar.activation(th[b][:, t, :], lo[:], ACT.Tanh, scale=g_inv[:, slot : slot + 1])
 
         def join(b, half):
             h_bf[b, half] = held(f"h_bf{b}{half}", [P, HALF * PACK], BF16)
@@ -259,75 +262,74 @@ def tile_list_mentoring_pair_proposals_kernel(
             )
 
         def quantize_h(b, half):
-            h_w[b, half], h_s[b, half] = quantize(f"h{b}{half}", h_bf[b, half][:], HALF)
+            if half == 0:
+                h_w[b] = held(f"h_w{b}", [P, S], U32)
+                h_s[b] = held(f"h_s{b}", [P, S], U8)
+            entries = slice(half * HALF, (half + 1) * HALF)
+            nc.vector.quantize_mx(out=h_w[b][:, entries].bitcast(FP8X4), scales=h_s[b][:, entries], in_=h_bf[b, half][:])
 
         frac = {}
 
-        def stage2(half, nt):
-            e = bank(f"e{half}{nt}")
-            for b in range(HP):
+        def last_product(half, nt):
+            entries = slice(half * HALF, (half + 1) * HALF)
+            e_bank = bank(f"e{half}{nt}")
+            e = e_bank[:, 0:HALF]
+            for b in range(R_PASSES):
                 nc.tensor.matmul_mx(
-                    out=e[:, 0:HALF],
+                    out=e,
                     lhsT=wc_w[nt][:, b * P : (b + 1) * P].bitcast(FP8X4),
                     lhsT_scale=wc_s[nt][:, b * P : (b + 1) * P],
-                    rhs=h_w[b, half][:].bitcast(FP8X4),
-                    rhs_scale=h_s[b, half][:],
+                    rhs=h_w[b][:, entries].bitcast(FP8X4),
+                    rhs_scale=h_s[b][:, entries],
                     start=(b == 0),
-                    stop=(b == HP - 1),
+                    stop=(b == R_PASSES - 1),
                 )
             shifted = ring.tile([P, HALF], U32, name="shifted")
             whole = ring.tile([P, HALF], F32, name="whole")
             frac[half, nt] = ring.tile([P, HALF], F32, name="frac")
-            nc.scalar.activation(shifted[:], e[:, 0:HALF], ACT.Copy, bias=ROUNDER, scale=turns[:, nt : nt + 1])
+            nc.scalar.activation(shifted[:], e, ACT.Copy, bias=ROUNDER, scale=turns[:, nt : nt + 1])
             nc.scalar.activation(whole[:], shifted[:], ACT.Copy, bias=-ROUNDER)
-            nc.vector.scalar_tensor_tensor(frac[half, nt][:], e[:, 0:HALF], turns[:, nt : nt + 1], whole[:], ALU.mult, ALU.subtract)
+            nc.vector.scalar_tensor_tensor(frac[half, nt][:], e, turns[:, nt : nt + 1], whole[:], ALU.mult, ALU.subtract)
 
         def place(half, nt):
             y = ring.tile([P, HALF], F32, name="y")
             nc.scalar.activation(y[:], frac[half, nt][:], ACT.Sin, scale=2.0 * math.pi)
-            places = idx3[:, half * (HALF // 16) : (half + 1) * (HALF // 16)]
+            places = idx3[:, half * HALF // LIST_ROWS : (half + 1) * HALF // LIST_ROWS]
             nc.vector.tensor_tensor(
                 pages[nt][:].indirect(places), y[:], wgo_sb[:, half * HALF : (half + 1) * HALF], ALU.mult
             )
 
-        def prepare(unit):
-            b, t = divmod(unit, PACK)
-            if t == 0:
-                deal_wb(b)
-                prepare_first_pass(b, nc.vector.tensor_copy if b == 0 else nc.scalar.copy)
-            prepare_second_pass(b, t, nc.vector.tensor_copy if unit == 0 else nc.scalar.copy)
-
         prepare(0)
-        for unit in range(HP * PACK):
-            if unit + 1 < HP * PACK:
-                prepare(unit + 1)
-            stage1(*divmod(unit, PACK))
-            if unit == 4:
+        for slot in range(SLOTS):
+            if slot + 1 < SLOTS:
+                prepare(slot + 1)
+            first_products(slot)
+            if slot == PACK:
                 join(0, 0)
-            if unit == 5:
+            if slot == PACK + 1:
                 quantize_h(0, 0)
                 join(0, 1)
-            if unit == 6:
+            if slot == PACK + 2:
                 quantize_h(0, 1)
                 round_wc(0)
-        cols2 = bank("cols2")
-        nc.tensor.transpose(cols2[:, 0:P], rows2[:], ident[:])
-        nc.scalar.activation(turns[:], cols2[:, 0:NT], ACT.Copy, scale=1.0 / (2.0 * math.pi))
-        quantize_wc(0)
-        round_wc(1)
+        stretch_bank = bank("stretch_bank")
+        nc.tensor.transpose(stretch_bank[:, 0:P], rows[:, 0:P], ident[:])
+        nc.scalar.activation(
+            turns[:], stretch_bank[:, R_PASSES : R_PASSES + N_TILES], ACT.Copy, scale=1.0 / (2.0 * math.pi)
+        )
         join(1, 0)
-        quantize_wc(1)
+        quantize_wc(0)
         quantize_h(1, 0)
         join(1, 1)
-        pieces = [(half, nt) for half in range(2) for nt in range(NT)]
-        stage2(*pieces[0])
+        pieces = [(half, nt) for half in range(2) for nt in range(N_TILES)]
+        last_product(*pieces[0])
         quantize_h(1, 1)
-        for n, (half, nt) in enumerate(pieces):
-            if n + 2 < NT:
-                round_wc(n + 2)
-                quantize_wc(n + 2)
-            if n + 1 < len(pieces):
-                stage2(*pieces[n + 1])
+        for step, (half, nt) in enumerate(pieces):
+            if step + 1 < N_TILES:
+                round_wc(step + 1)
+                quantize_wc(step + 1)
+            if step + 1 < len(pieces):
+                last_product(*pieces[step + 1])
             place(half, nt)
             if half == 1:
                 nc.sync.dma_start(out=out[nt * P : (nt + 1) * P, :], in_=pages[nt][:])

import math
from contextlib import ExitStack

import concourse.mybir as mybir
from concourse.masks import make_identity

K, T, S, H, N, T2 = 1024, 2048, 512, 1024, 512, 1024
FLOPS = 2 * S * (2 * K * H + H * N)

F32 = mybir.dt.float32
BF16 = mybir.dt.bfloat16
I32 = mybir.dt.int32
U32 = mybir.dt.uint32
U16 = mybir.dt.uint16
U8 = mybir.dt.uint8
FP8X4 = mybir.dt.float8_e4m3fn_x4
FP4X4 = mybir.dt.float4_e2m1fn_x4
ALU = mybir.AluOpType
ACT = mybir.ActivationFunctionType

P = 128
PACK = 4
PASS = P * PACK
K_PASSES = K // PASS
R_PASSES = H // PASS
SLOTS = R_PASSES * PACK
N_TILES = N // P
HALF = S // 2
RUN = 8
BLOCKS = PASS // 32
QUADRANTS = 4
SCALE_ROWS = 4
LIST_ROWS = 16
LAST_SCALE_ROW = 32 * (QUADRANTS - 1) + SCALE_ROWS
VECTOR_PAGES = 2
TOR_BUFS = PACK + 1
ROUNDER = 1.5 * 2.0**23
TINY = 2.0**-100


def tile_list_mentoring_pair_proposals_kernel(
    tc, tab_words, tab_scales, offs, offs2, wa, wb_words, wb_scales, gain, wc, stretch, wgo, offs3, out
):
    nc = tc.nc
    with ExitStack() as ctx:
        keep = ctx.enter_context(tc.tile_pool(name="keep", bufs=1))
        ring = ctx.enter_context(tc.tile_pool(name="ring", bufs=3))
        psum = ctx.enter_context(tc.psum_pool(name="psum", bufs=8))

        def held(name, shape, dtype, tag=""):
            return keep.tile(shape, dtype, name=name, tag=tag or name, align_bytes=64)

        def bank(name):
            return psum.tile([P, S], F32, name=name, tag="bank")

        idx = held("idx", [P, S // LIST_ROWS], U16)
        idx2 = held("idx2", [P, S // LIST_ROWS], U16)
        idx3 = held("idx3", [P, S // LIST_ROWS], U16)
        tab_w = [held(f"tab_w{a}", [P, T], I32) for a in range(K_PASSES)]
        tab_s = held("tab_s", [P, T // 4], I32)
        wb_s_raw = held("wb_s_raw", [P, K_PASSES * H // 4], I32)
        v2_s_last = held("v2_s_last", [P, S // 4], I32)
        gain_rows = held("gain_rows", [R_PASSES, PASS], F32)
        rows = held("rows", [P, PACK * P], F32)
        ident = held("ident", [P, P], F32)
        pages = [held(f"page{nt}", [P, T2], F32) for nt in range(N_TILES)]

        nc.gpsimd.memset(tab_s[:], 0)
        make_identity(nc, ident[:])
        nc.vector.memset(wb_s_raw[:], 0)
        nc.vector.memset(rows[:], 0.0)
        nc.vector.memset(v2_s_last[:], 0)
        for nt, page in enumerate(pages):
            (nc.vector if nt < VECTOR_PAGES else nc.gpsimd).memset(page[:], 0.0)

        warm = held("warm", [P, 1], F32)
        nc.scalar.activation(warm[:], ident[:, 0:1], ACT.Silu)

        wa_raw, wb_raw, wc_raw = {}, {}, {}

        def load_table(a):
            nc.sync.dma_start(out=tab_w[a][:], in_=tab_words[a].rearrange("p t i -> p (t i)").bitcast(I32))

        def load_wa(a, b):
            wa_raw[a, b] = held(f"wa_raw{a}{b}", [P, PACK, PASS], F32)
            nc.sync.dma_start(
                out=wa_raw[a, b][:],
                in_=wa[a * PASS : (a + 1) * PASS, b * PASS : (b + 1) * PASS].rearrange("(p j) c -> p j c", j=PACK),
            )

        def load_wb(b):
            wb_raw[b] = held(f"wb_raw{b}", [P, K_PASSES, PASS // 2], I32)
            nc.sync.dma_start(
                out=wb_raw[b][:],
                in_=wb_words.bitcast(I32)[:, :, b * (PASS // 2) : (b + 1) * (PASS // 2)].rearrange("a p w -> p a w"),
            )

        def load_wc(b):
            wc_raw[b] = held(f"wc_raw{b}", [P, PACK, N], F32)
            by_code = wc[b * PASS : (b + 1) * PASS, :].rearrange("(q t i) n -> t q i n", t=PACK, i=RUN)
            for t in range(PACK):
                nc.sync.dma_start(out=wc_raw[b][:, t, :], in_=by_code[t])

        nc.sync.dma_start(idx2[:], offs2)
        nc.sync.dma_start(idx[:], offs)
        for quad in range(QUADRANTS):
            nc.sync.dma_start(
                out=tab_s[32 * quad : 32 * quad + SCALE_ROWS * K_PASSES, :],
                in_=tab_scales.bitcast(I32)[:, SCALE_ROWS * quad : SCALE_ROWS * (quad + 1), :],
            )
        load_table(0)
        load_table(1)
        v_s = held("v_s", [P, S], U8)
        v2_s = held("v2_s", [P, S], U8)
        nc.vector.tensor_copy(v2_s[:], tab_s[:].bitcast(U8).indirect(idx2[:]))
        nc.scalar.dma_start(
            out=v2_s_last[0:LAST_SCALE_ROW, :], in_=v2_s[SCALE_ROWS : SCALE_ROWS + LAST_SCALE_ROW, :].bitcast(I32)
        )
        nc.sync.dma_start(out=gain_rows[:], in_=gain.rearrange("(b c) -> b c", b=R_PASSES))
        load_wb(0)
        for quad in range(QUADRANTS):
            nc.sync.dma_start(
                out=wb_s_raw[32 * quad : 32 * quad + SCALE_ROWS, :].rearrange("r (a w) -> r a w", a=K_PASSES),
                in_=wb_scales.bitcast(I32)[:, SCALE_ROWS * quad : SCALE_ROWS * (quad + 1), :].rearrange("a r w -> r a w"),
            )
        load_wa(0, 0)
        load_wa(1, 0)
        load_wb(1)
        load_wa(0, 1)
        load_wa(1, 1)
        load_wc(0)
        load_wc(1)
        wgo_sb = held("wgo_sb", [P, S], F32)
        nc.sync.dma_start(out=wgo_sb[:], in_=wgo)
        nc.sync.dma_start(idx3[:], offs3)

        gain_bank = bank("gain_bank")
        nc.scalar.copy(
            out=rows[0:R_PASSES, :].rearrange("b (t q i) -> b t q i", t=PACK, i=RUN),
            in_=gain_rows[:].rearrange("b (q t i) -> b t q i", t=PACK, i=RUN),
        )
        for t in range(PACK):
            nc.tensor.transpose(gain_bank[:, t * P : (t + 1) * P], rows[:, t * P : (t + 1) * P], ident[:])
        g_cols = gain_bank[:].rearrange("p (t c) -> p c t", t=PACK)[:, 0:R_PASSES, :]
        nc.sync.dma_start(out=rows[R_PASSES : R_PASSES + N_TILES, 0:P], in_=stretch.rearrange("(c p) -> c p", p=P))
        g_abs = held("g_abs", [P, SLOTS], F32)
        g_sign = held("g_sign", [P, SLOTS], F32)
        turns = held("turns", [P, N_TILES], F32)
        g_mag = held("g_mag", [P, SLOTS], F32)
        g_rec = held("g_rec", [P, SLOTS], F32)
        g_inv = held("g_inv", [P, SLOTS], F32)
        nc.scalar.activation(g_abs[:].rearrange("p (b t) -> p b t", b=R_PASSES), g_cols, ACT.Abs)
        nc.scalar.activation(g_sign[:].rearrange("p (b t) -> p b t", b=R_PASSES), g_cols, ACT.Sign)
        nc.scalar.activation(g_mag[:], g_abs[:], ACT.Copy, bias=TINY)
        nc.vector.reciprocal(g_rec[:], g_mag[:])
        nc.vector.tensor_tensor(g_inv[:], g_rec[:], g_sign[:], ALU.mult)

        v_w = [held("v_w0", [P, S], U32)]
        v2_w = [held(f"v2_w{a}", [P, S], U32) for a in range(K_PASSES)]
        nc.vector.tensor_copy(v_s[:], tab_s[:].bitcast(U8).indirect(idx[:]))
        nc.vector.tensor_copy(v2_w[0][:], tab_w[0][:].bitcast(U32).indirect(idx2[:]))
        nc.vector.tensor_copy(v_w[0][:], tab_w[0][:].bitcast(U32).indirect(idx[:]))
        nc.vector.tensor_copy(v2_w[1][:], tab_w[1][:].bitcast(U32).indirect(idx2[:]))
        v2_scales = [v2_s[:], v2_s_last[:].bitcast(U8)]

        wb_s = held("wb_s", [P, K_PASSES * H], U8)
        nc.vector.tensor_copy(
            out=wb_s[:].bitcast(I32).rearrange("p (g t q w) -> p g t q w", t=PACK, q=BLOCKS, w=RUN // 4),
            in_=wb_s_raw[:].rearrange("p (g q t w) -> p g t q w", t=PACK, q=BLOCKS, w=RUN // 4),
        )
        v_w.append(held("v_w1", [P, S], U32, tag="wb_s_raw"))
        nc.vector.tensor_copy(v_w[1][:], tab_w[1][:].bitcast(U32).indirect(idx[:]))

        wb_w, wa_bf, wa_w, wa_s, wc_bf, wc_w, wc_s = {}, {}, {}, {}, {}, {}, {}

        def deal_wb(b):
            wb_w[b] = held(f"wb_w{b}", [P, K_PASSES * 2 * PASS], U8)
            nc.vector.tensor_copy(
                out=wb_w[b][:].bitcast(I32).rearrange("p (a t q w) -> p a t q w", a=K_PASSES, t=PACK, w=RUN // 2),
                in_=wb_raw[b][:].rearrange("p a (q t w) -> p a t q w", t=PACK, w=RUN // 2),
            )

        def quantize(name, src, width):
            words = held(name + "_w", [P, width], U32)
            scales = held(name + "_s", [P, width], U8)
            nc.vector.quantize_mx(out=words[:].bitcast(FP8X4), scales=scales[:], in_=src)
            return words, scales

        def round_wa(a, b, t, copy):
            wa_bf[a, b, t] = held(f"wa_bf{a}{b}{t}", [P, PASS], BF16)
            src = wa_raw[a, b][:].rearrange("p j (q t u e) -> p t q u j e", t=PACK, u=RUN // 4, e=4)
            copy(out=wa_bf[a, b, t][:].rearrange("p (q u e j) -> p q u j e", u=RUN // 4, e=4, j=PACK), in_=src[:, t])

        def quantize_wa(a, b, t):
            wa_w[a, b, t], wa_s[a, b, t] = quantize(f"wa{a}{b}{t}", wa_bf[a, b, t][:], P)

        def prepare(slot):
            b, t = divmod(slot, PACK)
            if t == 0:
                deal_wb(b)
            round_wa(0, b, t, nc.vector.tensor_copy if b == 0 else nc.scalar.copy)
            round_wa(1, b, t, nc.vector.tensor_copy if slot == 0 else nc.scalar.copy)
            for a in range(K_PASSES):
                quantize_wa(a, b, t)

        def round_wc(nt):
            wc_bf[nt] = held(f"wc_bf{nt}", [P, R_PASSES, PASS], BF16)
            for b in range(R_PASSES):
                nc.scalar.copy(
                    out=wc_bf[nt][:, b, :].rearrange("p (c e t) -> p c t e", e=4, t=PACK),
                    in_=wc_raw[b][:, :, nt * P : (nt + 1) * P].rearrange("p t (c e) -> p c t e", e=4),
                )

        def quantize_wc(nt):
            wc_w[nt], wc_s[nt] = quantize(f"wc{nt}", wc_bf[nt][:].rearrange("p b c -> p (b c)"), R_PASSES * P)

        hi, th, h_bf, h_w, h_s = {}, {}, {}, {}, {}

        def first_products(slot):
            b, t = divmod(slot, PACK)
            if t == 0:
                hi[b] = held(f"hi{b}", [P, PACK, S], F32)
                th[b] = held(f"th{b}", [P, PACK, S], F32)
            mag = g_mag[:, slot : slot + 1]
            tor = bank(f"tor{slot}")
            for a in range(K_PASSES):
                nc.tensor.matmul_mx(
                    out=tor[:],
                    lhsT=wb_w[b][:, (a * PACK + t) * 2 * P : (a * PACK + t + 1) * 2 * P].bitcast(FP4X4),
                    lhsT_scale=wb_s[:, a * H + slot * P : a * H + (slot + 1) * P],
                    rhs=v2_w[a][:].bitcast(FP8X4),
                    rhs_scale=v2_scales[a],
                    start=(a == 0),
                    stop=(a == K_PASSES - 1),
                )
            tor_g = ring.tile([P, S], F32, name="tor_g", bufs=TOR_BUFS)
            nc.scalar.activation(tor_g[:], tor[:], ACT.Copy, scale=mag)
            ment = bank(f"ment{slot}")
            for a in range(K_PASSES):
                nc.tensor.matmul_mx(
                    out=ment[:],
                    lhsT=wa_w[a, b, t][:].bitcast(FP8X4),
                    lhsT_scale=wa_s[a, b, t][:],
                    rhs=v_w[a][:].bitcast(FP8X4),
                    rhs_scale=v_s[SCALE_ROWS * a : P, :],
                    start=(a == 0),
                    stop=(a == K_PASSES - 1),
                )
            lo = ring.tile([P, S], F32, name="lo")
            nc.vector.scalar_tensor_tensor(lo[:], ment[:], mag, tor_g[:], ALU.mult, ALU.min)
            nc.vector.scalar_tensor_tensor(hi[b][:, t, :], ment[:], mag, tor_g[:], ALU.mult, ALU.max)
            nc.scalar.activation(th[b][:, t, :], lo[:], ACT.Tanh, scale=g_inv[:, slot : slot + 1])

        def join(b, half):
            h_bf[b, half] = held(f"h_bf{b}{half}", [P, HALF * PACK], BF16)
            entries = slice(half * HALF, (half + 1) * HALF)
            nc.vector.tensor_tensor(
                h_bf[b, half][:].rearrange("p (c e t) -> p c t e", e=2, t=PACK),
                hi[b][:, :, entries].rearrange("p t (c e) -> p c t e", e=2),
                th[b][:, :, entries].rearrange("p t (c e) -> p c t e", e=2),
                ALU.mult,
            )

        def quantize_h(b, half):
            if half == 0:
                h_w[b] = held(f"h_w{b}", [P, S], U32)
                h_s[b] = held(f"h_s{b}", [P, S], U8)
            entries = slice(half * HALF, (half + 1) * HALF)
            nc.vector.quantize_mx(out=h_w[b][:, entries].bitcast(FP8X4), scales=h_s[b][:, entries], in_=h_bf[b, half][:])

        frac = {}

        def last_product(half, nt):
            entries = slice(half * HALF, (half + 1) * HALF)
            e_bank = bank(f"e{half}{nt}")
            e = e_bank[:, 0:HALF]
            for b in range(R_PASSES):
                nc.tensor.matmul_mx(
                    out=e,
                    lhsT=wc_w[nt][:, b * P : (b + 1) * P].bitcast(FP8X4),
                    lhsT_scale=wc_s[nt][:, b * P : (b + 1) * P],
                    rhs=h_w[b][:, entries].bitcast(FP8X4),
                    rhs_scale=h_s[b][:, entries],
                    start=(b == 0),
                    stop=(b == R_PASSES - 1),
                )
            shifted = ring.tile([P, HALF], U32, name="shifted")
            whole = ring.tile([P, HALF], F32, name="whole")
            frac[half, nt] = ring.tile([P, HALF], F32, name="frac")
            nc.scalar.activation(shifted[:], e, ACT.Copy, bias=ROUNDER, scale=turns[:, nt : nt + 1])
            nc.scalar.activation(whole[:], shifted[:], ACT.Copy, bias=-ROUNDER)
            nc.vector.scalar_tensor_tensor(frac[half, nt][:], e, turns[:, nt : nt + 1], whole[:], ALU.mult, ALU.subtract)

        def place(half, nt):
            y = ring.tile([P, HALF], F32, name="y")
            nc.scalar.activation(y[:], frac[half, nt][:], ACT.Sin, scale=2.0 * math.pi)
            places = idx3[:, half * HALF // LIST_ROWS : (half + 1) * HALF // LIST_ROWS]
            nc.vector.tensor_tensor(
                pages[nt][:].indirect(places), y[:], wgo_sb[:, half * HALF : (half + 1) * HALF], ALU.mult
            )

        prepare(0)
        for slot in range(SLOTS):
            if slot + 1 < SLOTS:
                prepare(slot + 1)
            first_products(slot)
            if slot == PACK:
                join(0, 0)
            if slot == PACK + 1:
                quantize_h(0, 0)
                join(0, 1)
            if slot == PACK + 2:
                quantize_h(0, 1)
                round_wc(0)
        stretch_bank = bank("stretch_bank")
        nc.tensor.transpose(stretch_bank[:, 0:P], rows[:, 0:P], ident[:])
        nc.scalar.activation(
            turns[:], stretch_bank[:, R_PASSES : R_PASSES + N_TILES], ACT.Copy, scale=1.0 / (2.0 * math.pi)
        )
        join(1, 0)
        quantize_wc(0)
        quantize_h(1, 0)
        join(1, 1)
        pieces = [(half, nt) for half in range(2) for nt in range(N_TILES)]
        last_product(*pieces[0])
        quantize_h(1, 1)
        for step, (half, nt) in enumerate(pieces):
            if step + 1 < N_TILES:
                round_wc(step + 1)
                quantize_wc(step + 1)
            if step + 1 < len(pieces):
                last_product(*pieces[step + 1])
            place(half, nt)
            if half == 1:
                nc.sync.dma_start(out=out[nt * P : (nt + 1) * P, :], in_=pages[nt][:])
